import numpy as np
import ml_dtypes


def mxq(x, axis, fmt="e4m3"):
    dtype, down = {"e4m3": (ml_dtypes.float8_e4m3fn, 7), "e5m2": (ml_dtypes.float8_e5m2, 14)}[fmt]
    v = np.moveaxis(np.asarray(x, np.float32).astype(ml_dtypes.bfloat16).astype(np.float64), axis, -1)
    blocks = v.reshape(v.shape[:-1] + (-1, 32))
    amax = np.abs(blocks).max(-1, keepdims=True)
    byte = np.maximum(np.where(amax > 0, np.frexp(amax)[1] - 1 + 127, 0) - down, 1)
    scale = np.exp2(byte - 127.0)
    codes = (blocks / scale).astype(np.float32).astype(dtype).astype(np.float64)
    return np.moveaxis((codes * scale).reshape(v.shape), -1, axis)


WIDE = False


def mx_kscale(k):
    if not WIDE:
        return np.ones(k)
    levels = np.array([10, -10, 5, -5, 0])
    if k % 512:
        return np.exp2(np.random.permutation(np.resize(levels, k // 32))).repeat(32)
    a = np.empty((k // 512, 16))
    for p in range(k // 512):
        a[p, :8] = np.random.permutation(np.resize(levels, 8))
        for g in range(8):
            far = levels[np.abs(levels - a[p, g]) >= 10]
            a[p, g + 8] = far[np.random.randint(len(far))]
    return np.exp2(a.ravel()).repeat(32)


def f64(x):
    return np.asarray(x).astype(np.float64)


def striped(idx):
    return np.tile(idx.reshape(-1, 16).T, (8, 1)).astype(np.uint16)


def unstriped(offs):
    return offs[:16].T.reshape(-1).astype(np.int64)


def striped8(idx):
    return np.concatenate([x.reshape(-1, 16).T for x in idx]).astype(np.uint16)


def runs(offs, k):
    lists = np.stack([offs[16 * r : 16 * r + 16].T.reshape(-1) for r in range(8)]).astype(np.int64)
    return lists[np.arange(k) % 512 // 64]


def pack_weight(w):
    k, n = w.shape
    w = f64(np.asarray(w, np.float32).astype(ml_dtypes.bfloat16)).reshape(k // 32, 32, n)
    amax = np.abs(w).max(1)
    byte = np.clip(np.where(amax > 0, np.frexp(amax)[1] - 1 + 127 - 7, 1), 1, 254)
    scaled = (w * np.exp2(127.0 - byte)[:, None, :]).reshape(k, n).astype(np.float32)
    words = np.ascontiguousarray(scaled.reshape(k // 512, 128, 4, n).transpose(0, 1, 3, 2)).astype(ml_dtypes.float8_e4m3fn).view(np.uint8)
    return words, np.ascontiguousarray(byte.astype(np.uint8).reshape(k // 512, 16, n))


def unpack_weight(words, scales):
    g, p, n, _ = words.shape
    vals = np.ascontiguousarray(words).view(ml_dtypes.float8_e4m3fn).astype(np.float64) * np.repeat(np.exp2(scales.astype(np.float64) - 127.0), 8, axis=1)[..., None]
    return vals.transpose(0, 1, 3, 2).reshape(g * 512, n)


def sigmoid(v):
    return 1.0 / (1.0 + np.exp(-np.maximum(v, -700.0)))

def planes(y):
    n, m = y.shape
    v = y.astype(np.float32).astype(ml_dtypes.bfloat16).astype(np.float64).reshape(n // 32, 32, m)
    top = np.abs(v).max(1)
    byte = np.clip(np.where(top > 0, np.frexp(top)[1] - 1 + 127 - 7, 1), 1, 254)
    codes = (v * np.exp2(127.0 - byte)[:, None, :]).reshape(n, m).astype(np.float32).astype(ml_dtypes.float8_e4m3fn).view(np.uint8)
    words = codes.reshape(n // 512, 128, 4, m).transpose(0, 1, 3, 2)
    return np.ascontiguousarray(words), np.ascontiguousarray(byte.astype(np.uint8).reshape(n // 512, 16, m))


K, T, S, G, H, C = 512, 1024, 256, 2048, 512, 512


def setup_inputs():
    n = np.random.standard_normal
    s = mx_kscale(K)[:, None]
    packed_xT = pack_weight(n((K, T)) * s)
    packed_dT = pack_weight(n((K, G)) / s)
    return {
        "x_words": packed_xT[0],
        "x_scales": packed_xT[1],
        "d_words": packed_dT[0],
        "d_scales": packed_dT[1],
        "gs": (np.random.uniform(0.5, 1.5, (K, 1)) / s).astype(np.float32),
        "offs": striped(np.random.permutation(T)[:S]),
        "k1": striped8(np.random.randint(0, G, (8, H))),
        "n1": striped8(np.stack([np.random.permutation(S) for _ in range(8)])),
        "n2": striped8(np.stack([np.random.permutation(S) for _ in range(8)])),
        "cand": striped(np.random.permutation(T)[:C]),
        "two": striped(np.random.permutation(T)[:S]),
        "k2": striped8(np.random.randint(0, G, (8, H))),
        "n3": striped(np.random.permutation(S)),
        "n4": striped(np.random.permutation(S)),
    }


def reference(x_words, x_scales, d_words, d_scales, gs, offs, k1, n1, n2, cand, two, k2, n3, n4):
    x_cand = unpack_weight(x_words, x_scales)[:, unstriped(cand)]
    d_k1 = unpack_weight(d_words, d_scales)[np.arange(K)[:, None], runs(k1, K)]
    xq = unpack_weight(x_words, x_scales)[:, unstriped(offs)]
    h = 0.0625 * (d_k1.T @ xq)
    st = h * (sigmoid(h[np.arange(H)[:, None], runs(n1, H)]))
    z = f64(gs) * (st - (st[np.arange(H)[:, None], runs(n2, H)]))
    a = 0.0625 * ((x_cand.T @ mxq(z, 0, "e4m3")))
    d_k2 = unpack_weight(d_words, d_scales)[np.arange(K)[:, None], runs(k2, K)]
    x_two = unpack_weight(x_words, x_scales)[:, unstriped(two)]
    b = 0.0625 * (d_k2.T @ x_two)
    out_0 = (a - a[:, unstriped(n3)]) / (np.abs(b) + np.abs(b[:, unstriped(n4)]) + 0.5)
    return (out_0,) + planes(out_0)

@@ -1,0 +1,204 @@
+from contextlib import ExitStack
+
+import concourse.mybir as mybir
+
+K, T, S, G, H, C = 512, 1024, 256, 2048, 512, 512
+FLOPS = 3 * 2 * K * H * S
+
+F32 = mybir.dt.float32
+BF16 = mybir.dt.bfloat16
+I32 = mybir.dt.int32
+U32 = mybir.dt.uint32
+U16 = mybir.dt.uint16
+U8 = mybir.dt.uint8
+FP8X4 = mybir.dt.float8_e4m3fn_x4
+ACT = mybir.ActivationFunctionType
+ALU = mybir.AluOpType
+
+P = 128
+PACK = 4
+QUAD = 32
+SHIFT = 14
+SPAN = 3 * QUAD + PACK
+WIN = 2 * S
+SIXTEENTH = 0.0625
+
+
+def tile_picked_pqcjnormbhopg_none_po_kernel(
+    tc, x_words, x_scales, d_words, d_scales, gs, offs, k1, n1, n2, cand, two, k2, n3, n4, out_0, out_1, out_2
+):
+    nc = tc.nc
+    with ExitStack() as ctx:
+        lists = ctx.enter_context(tc.tile_pool(name="lists", bufs=1))
+        sb = ctx.enter_context(tc.tile_pool(name="sb", bufs=1))
+        ps = ctx.enter_context(tc.psum_pool(name="ps", bufs=1))
+
+        def load_list(src, name):
+            dst = lists.tile([P, src.shape[1]], U16, name=name)
+            nc.sync.dma_start(dst[:], src)
+            return dst
+
+        dw = sb.tile([P, G], I32, name="dw", align_bytes=64)
+        xw = sb.tile([P, T], I32, name="xw", align_bytes=64)
+        ds = sb.tile([P, G], U8, name="ds", align_bytes=64)
+        xs = sb.tile([P, T], U8, name="xs", align_bytes=64)
+        k1_l = load_list(k1, "k1_l")
+        ds_rows = d_scales[0].bitcast(I32)
+        nc.sync.dma_start(ds[:].bitcast(I32), ds_rows.unsqueeze(1).to_broadcast([16, 8, G // 4]))
+        xs_rows = x_scales[0].bitcast(I32)
+
+        def load_xs(q, queue):
+            rows = xs_rows[PACK * q : PACK * (q + 1), :].unsqueeze(0).to_broadcast([8, PACK, T // 4])
+            queue.dma_start(xs[QUAD * q : QUAD * (q + 1), :].bitcast(I32), rows)
+
+        nc.scalar.dma_start(xw[:], x_words[0].rearrange("p n t -> p (n t)").bitcast(I32))
+        load_xs(0, nc.scalar)
+        nc.scalar.dma_start(dw[:], d_words[0].rearrange("p n t -> p (n t)").bitcast(I32))
+        offs_l = load_list(offs, "offs_l")
+        for q in range(1, PACK):
+            load_xs(q, nc.sync)
+        n1_l = load_list(n1, "n1_l")
+        k2_l = load_list(k2, "k2_l")
+        two_l = load_list(two, "two_l")
+        n2_l = load_list(n2, "n2_l")
+        cand_l = load_list(cand, "cand_l")
+        n4_l = load_list(n4, "n4_l")
+        n3_l = load_list(n3, "n3_l")
+
+        gs_t = sb.tile([P, PACK], F32, name="gs_t")
+        nc.gpsimd.dma_start(gs_t[:], gs.rearrange("(p t) o -> p (t o)", t=PACK))
+        gs16 = sb.tile([P, PACK], F32, name="gs16")
+        nc.gpsimd.tensor_scalar(gs16[:], gs_t[:], SIXTEENTH, 0.0, ALU.mult, ALU.add)
+
+        placed = {}
+        for name in ("k1", "k2"):
+            placed[name] = sb.tile([P, H], U8, name="placed_" + name, align_bytes=64)
+            nc.vector.memset(placed[name][:].bitcast(I32), 0)
+        sig = [sb.tile([P, WIN], F32, name="sig%d" % t, tag="sig%d" % t, align_bytes=64) for t in range(PACK)]
+        for t in range(PACK):
+            nc.vector.memset(sig[t][:, S:], 0.0)
+        b_abs = sb.tile([P, (PACK + 1) * S], F32, name="b_abs")
+        a_all = sb.tile([P, (PACK + 1) * S], F32, name="a_all")
+        nc.vector.memset(b_abs[:, PACK * S :], 0.0)
+        nc.vector.memset(a_all[:, PACK * S :], 0.0)
+
+        def gather_words(table, offsets, n, name, tag):
+            got = sb.tile([P, n], I32, name=name, tag=tag, align_bytes=64)
+            nc.vector.tensor_copy(got[:].bitcast(U32), table[:].bitcast(U32).indirect(offsets[:]))
+            return got
+
+        def gather_bytes(table, offsets, n, name, tag):
+            got = sb.tile([P, n], U8, name=name, tag=tag, align_bytes=64)
+            nc.vector.tensor_copy(got[:], table[:].indirect(offsets[:]))
+            return got
+
+        def deal(got, dtype, run, name):
+            dealt = sb.tile([P, H], dtype, name=name, align_bytes=64)
+            nc.vector.tensor_copy(
+                dealt[:].rearrange("p (t c i) -> p c t i", t=PACK, i=run),
+                got[:].rearrange("p (c i t) -> p c t i", t=PACK, i=run),
+            )
+            return dealt
+
+        def coded_scales(offsets, name, queue, tag):
+            dealt = deal(gather_bytes(ds, offsets, H, "gs_" + name, tag), U8, 16, "dealt_s_" + name)
+            for i in range(PACK):
+                queue.dma_start(placed[name][i:P:QUAD, :].bitcast(I32), dealt[8 * i : P : QUAD, :].bitcast(I32))
+            return placed[name]
+
+        def product(acc, w_words, w_scales, t, m_words, m_scales):
+            cols = slice(P * t, P * (t + 1))
+            nc.tensor.matmul_mx(
+                out=acc,
+                lhsT=w_words[:, cols].bitcast(FP8X4),
+                lhsT_scale=w_scales[:, cols],
+                rhs=m_words[:].bitcast(FP8X4),
+                rhs_scale=m_scales[:],
+                start=True,
+                stop=True,
+            )
+
+        def weave(dst, src):
+            nc.vector.tensor_copy(
+                dst[:].rearrange("p (c i t) -> p c t i", t=PACK, i=4),
+                src[:].rearrange("p (t c i) -> p c t i", t=PACK, i=4),
+            )
+
+        k1_s = coded_scales(k1_l, "k1", nc.scalar, "gs_k1")
+        xq_w = gather_words(xw, offs_l, S, "xq_w", "xq_w")
+        k1_w = deal(gather_words(dw, k1_l, H, "gw_k1", "gw_k1"), I32, 4, "dealt_w_k1")
+        xq_s = gather_bytes(xs, offs_l, S, "xq_s", "xq_s")
+        h_ps = [ps.tile([P, S], F32, name="h_ps%d" % t) for t in range(PACK)]
+        for t in range(PACK):
+            product(h_ps[t][:], k1_w, k1_s, t, xq_w, xq_s)
+
+        st = [sb.tile([P, WIN], F32, name="st%d" % t, tag="st%d" % t, align_bytes=64) for t in range(PACK)]
+        for t in range(PACK):
+            nc.scalar.activation(sig[t][:, :S], h_ps[t][:], ACT.Sigmoid, scale=SIXTEENTH)
+            nc.scalar.activation(st[t][:, S:], sig[t][:].indirect(n1_l[:]), ACT.Copy)
+            nc.vector.scalar_tensor_tensor(st[t][:, :S], h_ps[t][:], gs16[:, t : t + 1], st[t][:, S:], ALU.mult, ALU.mult)
+
+        k2_s = coded_scales(k2_l, "k2", nc.sync, "gw_k1")
+        k2_w = deal(gather_words(dw, k2_l, H, "gw_k2", "sig0"), I32, 4, "dealt_w_k2")
+        x2_w = gather_words(xw, two_l, S, "x2_w", "sig2")
+        x2_s = gather_bytes(xs, two_l, S, "x2_s", "sig3")
+        b_ps = [ps.tile([P, 2 * S], F32, name="b_ps%d" % u) for u in range(2)]
+        for t in range(PACK):
+            product(b_ps[t // 2][:, S * (t % 2) : S * (t % 2 + 1)], k2_w, k2_s, t, x2_w, x2_s)
+
+        st_n2 = sb.tile([P, PACK * S], F32, name="st_n2")
+        z_rows = sb.tile([P, PACK * S], BF16, name="z_rows")
+        for t in range(PACK):
+            cols = slice(S * t, S * (t + 1))
+            nc.scalar.activation(st_n2[:, cols], st[t][:].indirect(n2_l[:]), ACT.Copy)
+            nc.vector.tensor_tensor(z_rows[:, cols], st[t][:, :S], st_n2[:, cols], ALU.subtract)
+
+        cand_s = deal(gather_bytes(xs, cand_l, C, "gs_cand", "st1"), U8, 16, "dealt_s_cand")
+        cand_w = deal(gather_words(xw, cand_l, C, "gw_cand", "st0"), I32, 4, "dealt_w_cand")
+
+        z_woven = sb.tile([P, PACK * S], BF16, name="z_woven", align_bytes=64)
+        weave(z_woven, z_rows)
+        z_w = sb.tile([P, S], I32, name="z_w", align_bytes=64)
+        z_s = sb.tile([P, S], U8, name="z_s", align_bytes=64)
+        nc.vector.quantize_mx(out=z_w[:].bitcast(FP8X4), scales=z_s[:], in_=z_woven[:])
+
+        b_n4 = sb.tile([P, PACK * S], F32, name="b_n4")
+        den = sb.tile([P, PACK * S], F32, name="den")
+        root = sb.tile([P, PACK * S], F32, name="root")
+        for u in range(2):
+            nc.scalar.activation(b_abs[:, 2 * S * u : 2 * S * (u + 1)], b_ps[u][:], ACT.Abs, scale=SIXTEENTH)
+        for t in range(PACK):
+            nc.scalar.activation(b_n4[:, S * t : S * (t + 1)], b_abs[:, S * t : S * t + WIN].indirect(n4_l[:]), ACT.Copy)
+        for u in range(2):
+            cols = slice(2 * S * u, 2 * S * (u + 1))
+            nc.vector.scalar_tensor_tensor(den[:, cols], b_abs[:, cols], 0.5, b_n4[:, cols], ALU.add, ALU.add)
+            nc.scalar.activation(root[:, cols], den[:, cols], ACT.Abs_reciprocal_sqrt)
+
+        a_ps = [ps.tile([P, 2 * S], F32, name="a_ps%d" % u) for u in range(2)]
+        for t in range(PACK):
+            product(a_ps[t // 2][:, S * (t % 2) : S * (t % 2 + 1)], cand_w, cand_s, t, z_w, z_s)
+        a_n3 = sb.tile([P, PACK * S], F32, name="a_n3")
+        diff = sb.tile([P, PACK * S], F32, name="diff")
+        res = sb.tile([P, PACK * S], F32, name="res")
+        half = sb.tile([P, PACK * S], F32, name="half")
+        out_rows = out_0.rearrange("(p t) j -> p t j", t=PACK)
+        for u in range(2):
+            nc.scalar.activation(a_all[:, 2 * S * u : 2 * S * (u + 1)], a_ps[u][:], ACT.Copy, scale=SIXTEENTH)
+        for t in range(PACK):
+            cols = slice(S * t, S * (t + 1))
+            nc.scalar.activation(a_n3[:, cols], a_all[:, S * t : S * t + WIN].indirect(n3_l[:]), ACT.Copy)
+            nc.vector.tensor_tensor(diff[:, cols], a_all[:, cols], a_n3[:, cols], ALU.subtract)
+            nc.vector.tensor_tensor(half[:, cols], diff[:, cols], root[:, cols], ALU.mult)
+            nc.vector.tensor_tensor(res[:, cols], half[:, cols], root[:, cols], ALU.mult)
+            nc.sync.dma_start(out_rows[:, t, :], res[:, cols])
+
+        res_woven = sb.tile([P, PACK * S], BF16, name="res_woven", align_bytes=64)
+        weave(res_woven, res)
+        res_w = sb.tile([P, S], I32, name="res_w", align_bytes=64)
+        res_s = sb.tile([P, S], U8, name="res_s", align_bytes=64)
+        nc.vector.quantize_mx(out=res_w[:].bitcast(FP8X4), scales=res_s[:], in_=res_woven[:])
+        nc.sync.dma_start(out_1[0].rearrange("p n t -> p (n t)").bitcast(I32), res_w[:])
+        scale_rows = out_2[0].bitcast(I32)
+        for q in range(PACK):
+            queue = nc.scalar if q % 2 == 0 else nc.sync
+            queue.dma_start(scale_rows[PACK * q : PACK * (q + 1), :], res_s[QUAD * q : QUAD * q + PACK, :].bitcast(I32))

@@ -16,12 +16,15 @@ ACT = mybir.ActivationFunctionType
 ALU = mybir.AluOpType
 
 P = 128
-PACK = 4
+SLOTS = 4
 QUAD = 32
-SHIFT = 14
-SPAN = 3 * QUAD + PACK
-WIN = 2 * S
+BLOCK_PARTS = 8
+SCALE_ROWS = K // 32
+WINDOW = 2 * S
+LINE = 16
 SIXTEENTH = 0.0625
+N4_ON_SCALAR = 3
+WEAVE_ON_VECTOR = 42
 
 
 def tile_picked_pqcjnormbhopg_none_po_kernel(
@@ -31,32 +34,38 @@ def tile_picked_pqcjnormbhopg_none_po_kernel(
     with ExitStack() as ctx:
         lists = ctx.enter_context(tc.tile_pool(name="lists", bufs=1))
         sb = ctx.enter_context(tc.tile_pool(name="sb", bufs=1))
+        shared = ctx.enter_context(tc.tile_pool(name="shared", bufs=1))
         ps = ctx.enter_context(tc.psum_pool(name="ps", bufs=1))
+
+        def slot(t, count=1):
+            return slice(S * t, S * (t + count))
 
         def load_list(src, name):
             dst = lists.tile([P, src.shape[1]], U16, name=name)
             nc.sync.dma_start(dst[:], src)
             return dst
 
-        dw = sb.tile([P, G], I32, name="dw", align_bytes=64)
-        xw = sb.tile([P, T], I32, name="xw", align_bytes=64)
-        ds = sb.tile([P, G], U8, name="ds", align_bytes=64)
-        xs = sb.tile([P, T], U8, name="xs", align_bytes=64)
+        d_w = sb.tile([P, G], I32, name="d_w", align_bytes=64)
+        x_w = sb.tile([P, T], I32, name="x_w", align_bytes=64)
+        d_s = sb.tile([P, G], U8, name="d_s", align_bytes=64)
+        x_s = sb.tile([P, T], U8, name="x_s", align_bytes=64)
+
         k1_l = load_list(k1, "k1_l")
-        ds_rows = d_scales[0].bitcast(I32)
-        nc.sync.dma_start(ds[:].bitcast(I32), ds_rows.unsqueeze(1).to_broadcast([16, 8, G // 4]))
-        xs_rows = x_scales[0].bitcast(I32)
+        d_rows = d_scales[0].bitcast(I32)
+        nc.sync.dma_start(d_s[:].bitcast(I32), d_rows.unsqueeze(1).to_broadcast([SCALE_ROWS, BLOCK_PARTS, G // 4]))
 
-        def load_xs(q, queue):
-            rows = xs_rows[PACK * q : PACK * (q + 1), :].unsqueeze(0).to_broadcast([8, PACK, T // 4])
-            queue.dma_start(xs[QUAD * q : QUAD * (q + 1), :].bitcast(I32), rows)
+        x_rows = x_scales[0].bitcast(I32)
 
-        nc.scalar.dma_start(xw[:], x_words[0].rearrange("p n t -> p (n t)").bitcast(I32))
-        load_xs(0, nc.scalar)
-        nc.scalar.dma_start(dw[:], d_words[0].rearrange("p n t -> p (n t)").bitcast(I32))
+        def load_x_scales(q, queue):
+            rows = x_rows[SLOTS * q : SLOTS * (q + 1), :].unsqueeze(0).to_broadcast([QUAD // SLOTS, SLOTS, T // 4])
+            queue.dma_start(x_s[QUAD * q : QUAD * (q + 1), :].bitcast(I32), rows)
+
+        nc.scalar.dma_start(x_w[:], x_words[0].rearrange("p n t -> p (n t)").bitcast(I32))
+        load_x_scales(0, nc.scalar)
+        nc.scalar.dma_start(d_w[:], d_words[0].rearrange("p n t -> p (n t)").bitcast(I32))
         offs_l = load_list(offs, "offs_l")
-        for q in range(1, PACK):
-            load_xs(q, nc.sync)
+        for q in range(1, SLOTS):
+            load_x_scales(q, nc.sync)
         n1_l = load_list(n1, "n1_l")
         k2_l = load_list(k2, "k2_l")
         two_l = load_list(two, "two_l")
@@ -65,140 +74,142 @@ def tile_picked_pqcjnormbhopg_none_po_kernel(
         n4_l = load_list(n4, "n4_l")
         n3_l = load_list(n3, "n3_l")
 
-        gs_t = sb.tile([P, PACK], F32, name="gs_t")
-        nc.gpsimd.dma_start(gs_t[:], gs.rearrange("(p t) o -> p (t o)", t=PACK))
-        gs16 = sb.tile([P, PACK], F32, name="gs16")
-        nc.gpsimd.tensor_scalar(gs16[:], gs_t[:], SIXTEENTH, 0.0, ALU.mult, ALU.add)
+        gs_raw = sb.tile([P, SLOTS], F32, name="gs_raw")
+        nc.gpsimd.dma_start(gs_raw[:], gs.rearrange("(p t) o -> p (t o)", t=SLOTS))
+        gs_16th = sb.tile([P, SLOTS], F32, name="gs_16th")
+        nc.gpsimd.tensor_scalar(gs_16th[:], gs_raw[:], SIXTEENTH, 0.0, ALU.mult, ALU.add)
 
-        placed = {}
-        for name in ("k1", "k2"):
-            placed[name] = sb.tile([P, H], U8, name="placed_" + name, align_bytes=64)
-            nc.vector.memset(placed[name][:].bitcast(I32), 0)
-        sig = [sb.tile([P, WIN], F32, name="sig%d" % t, tag="sig%d" % t, align_bytes=64) for t in range(PACK)]
-        for t in range(PACK):
+        k1_s = sb.tile([P, H], U8, name="k1_s", align_bytes=64)
+        k2_s = sb.tile([P, H], U8, name="k2_s", align_bytes=64)
+        nc.vector.memset(k1_s[:].bitcast(I32), 0)
+        nc.vector.memset(k2_s[:].bitcast(I32), 0)
+        sig = [sb.tile([P, WINDOW], F32, name="sig%d" % t, tag="sig%d" % t, align_bytes=64) for t in range(SLOTS)]
+        for t in range(SLOTS):
             nc.vector.memset(sig[t][:, S:], 0.0)
-        b_abs = sb.tile([P, (PACK + 1) * S], F32, name="b_abs")
-        a_all = sb.tile([P, (PACK + 1) * S], F32, name="a_all")
-        nc.vector.memset(b_abs[:, PACK * S :], 0.0)
-        nc.vector.memset(a_all[:, PACK * S :], 0.0)
+        b_abs = sb.tile([P, (SLOTS + 1) * S], F32, name="b_abs")
+        a_val = sb.tile([P, (SLOTS + 1) * S], F32, name="a_val")
+        nc.vector.memset(b_abs[:, slot(SLOTS)], 0.0)
+        nc.vector.memset(a_val[:, slot(SLOTS)], 0.0)
 
-        def gather_words(table, offsets, n, name, tag):
-            got = sb.tile([P, n], I32, name=name, tag=tag, align_bytes=64)
+        def gather_words(got, table, offsets):
             nc.vector.tensor_copy(got[:].bitcast(U32), table[:].bitcast(U32).indirect(offsets[:]))
             return got
 
-        def gather_bytes(table, offsets, n, name, tag):
-            got = sb.tile([P, n], U8, name=name, tag=tag, align_bytes=64)
+        def gather_bytes(got, table, offsets):
             nc.vector.tensor_copy(got[:], table[:].indirect(offsets[:]))
             return got
 
-        def deal(got, dtype, run, name):
+        def deal(got, dtype, per_line, name):
             dealt = sb.tile([P, H], dtype, name=name, align_bytes=64)
             nc.vector.tensor_copy(
-                dealt[:].rearrange("p (t c i) -> p c t i", t=PACK, i=run),
-                got[:].rearrange("p (c i t) -> p c t i", t=PACK, i=run),
+                dealt[:].rearrange("p (t c i) -> p c t i", t=SLOTS, i=per_line),
+                got[:].rearrange("p (c i t) -> p c t i", t=SLOTS, i=per_line),
             )
             return dealt
 
-        def coded_scales(offsets, name, queue, tag):
-            dealt = deal(gather_bytes(ds, offsets, H, "gs_" + name, tag), U8, 16, "dealt_s_" + name)
-            for i in range(PACK):
-                queue.dma_start(placed[name][i:P:QUAD, :].bitcast(I32), dealt[8 * i : P : QUAD, :].bitcast(I32))
-            return placed[name]
+        def place_scales(placed, dealt, queue):
+            for i in range(SLOTS):
+                queue.dma_start(placed[i:P:QUAD, :].bitcast(I32), dealt[BLOCK_PARTS * i : P : QUAD, :].bitcast(I32))
 
-        def product(acc, w_words, w_scales, t, m_words, m_scales):
-            cols = slice(P * t, P * (t + 1))
-            nc.tensor.matmul_mx(
-                out=acc,
-                lhsT=w_words[:, cols].bitcast(FP8X4),
-                lhsT_scale=w_scales[:, cols],
-                rhs=m_words[:].bitcast(FP8X4),
-                rhs_scale=m_scales[:],
-                start=True,
-                stop=True,
-            )
+        def product(acc, w_words, w_scales, m_words, m_scales):
+            for t in range(SLOTS):
+                cols = slice(P * t, P * (t + 1))
+                nc.tensor.matmul_mx(
+                    out=acc[t][:],
+                    lhsT=w_words[:, cols].bitcast(FP8X4),
+                    lhsT_scale=w_scales[:, cols],
+                    rhs=m_words[:].bitcast(FP8X4),
+                    rhs_scale=m_scales[:],
+                    start=True,
+                    stop=True,
+                )
 
-        def weave(dst, src):
-            nc.vector.tensor_copy(
-                dst[:].rearrange("p (c i t) -> p c t i", t=PACK, i=4),
-                src[:].rearrange("p (t c i) -> p c t i", t=PACK, i=4),
-            )
+        k1_s_got = gather_bytes(sb.tile([P, H], U8, name="k1_s_got", align_bytes=64), d_s, k1_l)
+        place_scales(k1_s, deal(k1_s_got, U8, LINE, "k1_s_dealt"), nc.scalar)
+        xq_w = gather_words(sb.tile([P, S], I32, name="xq_w", align_bytes=64), x_w, offs_l)
+        k1_w_got = gather_words(shared.tile([P, H], I32, name="k1_w_got", align_bytes=64, offset=0), d_w, k1_l)
+        k1_w = deal(k1_w_got, I32, LINE // 4, "k1_w")
+        xq_s = gather_bytes(sb.tile([P, S], U8, name="xq_s", align_bytes=64), x_s, offs_l)
+        h_ps = [ps.tile([P, S], F32, name="h_ps%d" % t, tag="h_ps%d" % t) for t in range(SLOTS)]
+        product(h_ps, k1_w, k1_s, xq_w, xq_s)
 
-        k1_s = coded_scales(k1_l, "k1", nc.scalar, "gs_k1")
-        xq_w = gather_words(xw, offs_l, S, "xq_w", "xq_w")
-        k1_w = deal(gather_words(dw, k1_l, H, "gw_k1", "gw_k1"), I32, 4, "dealt_w_k1")
-        xq_s = gather_bytes(xs, offs_l, S, "xq_s", "xq_s")
-        h_ps = [ps.tile([P, S], F32, name="h_ps%d" % t) for t in range(PACK)]
-        for t in range(PACK):
-            product(h_ps[t][:], k1_w, k1_s, t, xq_w, xq_s)
-
-        st = [sb.tile([P, WIN], F32, name="st%d" % t, tag="st%d" % t, align_bytes=64) for t in range(PACK)]
-        for t in range(PACK):
-            nc.scalar.activation(sig[t][:, :S], h_ps[t][:], ACT.Sigmoid, scale=SIXTEENTH)
+        st = [sb.tile([P, WINDOW], F32, name="st%d" % t, tag="st%d" % t, align_bytes=64) for t in range(SLOTS)]
+        nc.scalar.activation(sig[0][:, :S], h_ps[0][:], ACT.Sigmoid, scale=SIXTEENTH)
+        for t in range(SLOTS):
+            if t + 1 < SLOTS:
+                nc.scalar.activation(sig[t + 1][:, :S], h_ps[t + 1][:], ACT.Sigmoid, scale=SIXTEENTH)
             nc.scalar.activation(st[t][:, S:], sig[t][:].indirect(n1_l[:]), ACT.Copy)
-            nc.vector.scalar_tensor_tensor(st[t][:, :S], h_ps[t][:], gs16[:, t : t + 1], st[t][:, S:], ALU.mult, ALU.mult)
+            nc.vector.scalar_tensor_tensor(st[t][:, :S], h_ps[t][:], gs_16th[:, t : t + 1], st[t][:, S:], ALU.mult, ALU.mult)
 
-        k2_s = coded_scales(k2_l, "k2", nc.sync, "gw_k1")
-        k2_w = deal(gather_words(dw, k2_l, H, "gw_k2", "sig0"), I32, 4, "dealt_w_k2")
-        x2_w = gather_words(xw, two_l, S, "x2_w", "sig2")
-        x2_s = gather_bytes(xs, two_l, S, "x2_s", "sig3")
-        b_ps = [ps.tile([P, 2 * S], F32, name="b_ps%d" % u) for u in range(2)]
-        for t in range(PACK):
-            product(b_ps[t // 2][:, S * (t % 2) : S * (t % 2 + 1)], k2_w, k2_s, t, x2_w, x2_s)
+        k2_s_got = gather_bytes(shared.tile([P, H], U8, name="k2_s_got", align_bytes=64, offset=0), d_s, k2_l)
+        place_scales(k2_s, deal(k2_s_got, U8, LINE, "k2_s_dealt"), nc.sync)
+        x2_s = gather_bytes(shared.tile([P, S], U8, name="x2_s", align_bytes=64, offset=H), x_s, two_l)
+        x2_w = gather_words(shared.tile([P, S], I32, name="x2_w", align_bytes=64, offset=2 * H), x_w, two_l)
+        k2_w_got = gather_words(sb.tile([P, H], I32, name="k2_w_got", tag="sig0", align_bytes=64), d_w, k2_l)
+        k2_w = deal(k2_w_got, I32, LINE // 4, "k2_w")
+        b_ps = [ps.tile([P, S], F32, name="b_ps%d" % t) for t in range(SLOTS)]
+        product(b_ps, k2_w, k2_s, x2_w, x2_s)
 
-        st_n2 = sb.tile([P, PACK * S], F32, name="st_n2")
-        z_rows = sb.tile([P, PACK * S], BF16, name="z_rows")
-        for t in range(PACK):
-            cols = slice(S * t, S * (t + 1))
-            nc.scalar.activation(st_n2[:, cols], st[t][:].indirect(n2_l[:]), ACT.Copy)
-            nc.vector.tensor_tensor(z_rows[:, cols], st[t][:, :S], st_n2[:, cols], ALU.subtract)
+        st_n2 = sb.tile([P, SLOTS * S], F32, name="st_n2")
+        z_woven = sb.tile([P, SLOTS * S], BF16, name="z_woven", align_bytes=64)
+        z_slots = z_woven[:].rearrange("p (j t) -> p t j", t=SLOTS)
+        for t in range(SLOTS):
+            nc.scalar.activation(st_n2[:, slot(t)], st[t][:].indirect(n2_l[:]), ACT.Copy)
+            nc.gpsimd.tensor_tensor(z_slots[:, t, :], st[t][:, :S], st_n2[:, slot(t)], ALU.subtract)
 
-        cand_s = deal(gather_bytes(xs, cand_l, C, "gs_cand", "st1"), U8, 16, "dealt_s_cand")
-        cand_w = deal(gather_words(xw, cand_l, C, "gw_cand", "st0"), I32, 4, "dealt_w_cand")
-
-        z_woven = sb.tile([P, PACK * S], BF16, name="z_woven", align_bytes=64)
-        weave(z_woven, z_rows)
+        cand_s_got = gather_bytes(sb.tile([P, C], U8, name="cand_s_got", tag="st1", align_bytes=64), x_s, cand_l)
+        cand_s = deal(cand_s_got, U8, LINE, "cand_s")
+        cand_w = sb.tile([P, C], I32, name="cand_w", tag="st0", align_bytes=64)
+        nc.vector.tensor_copy(
+            cand_w[:].bitcast(U32).rearrange("p (t m) -> p m t", t=SLOTS), x_w[:].bitcast(U32).indirect(cand_l[:])
+        )
         z_w = sb.tile([P, S], I32, name="z_w", align_bytes=64)
         z_s = sb.tile([P, S], U8, name="z_s", align_bytes=64)
         nc.vector.quantize_mx(out=z_w[:].bitcast(FP8X4), scales=z_s[:], in_=z_woven[:])
+        a_ps = [ps.tile([P, S], F32, name="a_ps%d" % t, tag="h_ps%d" % t) for t in range(SLOTS)]
+        product(a_ps, cand_w, cand_s, z_w, z_s)
 
-        b_n4 = sb.tile([P, PACK * S], F32, name="b_n4")
-        den = sb.tile([P, PACK * S], F32, name="den")
-        root = sb.tile([P, PACK * S], F32, name="root")
-        for u in range(2):
-            nc.scalar.activation(b_abs[:, 2 * S * u : 2 * S * (u + 1)], b_ps[u][:], ACT.Abs, scale=SIXTEENTH)
-        for t in range(PACK):
-            nc.scalar.activation(b_n4[:, S * t : S * (t + 1)], b_abs[:, S * t : S * t + WIN].indirect(n4_l[:]), ACT.Copy)
-        for u in range(2):
-            cols = slice(2 * S * u, 2 * S * (u + 1))
-            nc.vector.scalar_tensor_tensor(den[:, cols], b_abs[:, cols], 0.5, b_n4[:, cols], ALU.add, ALU.add)
-            nc.scalar.activation(root[:, cols], den[:, cols], ACT.Abs_reciprocal_sqrt)
+        b_n4 = [sb.tile([P, S], F32, name="b_n4_%d" % t) for t in range(SLOTS)]
+        den = [sb.tile([P, 2 * S], F32, name="den%d" % u, tag="den%d" % u) for u in range(2)]
+        root = sb.tile([P, SLOTS * S], F32, name="root")
+        recip = sb.tile([P, SLOTS * S], F32, name="recip")
+        for t in range(SLOTS):
+            nc.scalar.activation(b_abs[:, slot(t)], b_ps[t][:], ACT.Abs, scale=SIXTEENTH)
+        for t in range(SLOTS):
+            looked_up = b_abs[:, slot(t, 2)].indirect(n4_l[:])
+            if t < N4_ON_SCALAR:
+                nc.scalar.activation(b_n4[t][:], looked_up, ACT.Copy)
+            else:
+                nc.vector.tensor_copy(b_n4[t][:], looked_up)
+            nc.vector.tensor_tensor(den[t // 2][:, slot(t % 2)], b_abs[:, slot(t)], b_n4[t][:], ALU.add)
+        for u, squarer in enumerate((nc.vector, nc.gpsimd)):
+            pair = slot(2 * u, 2)
+            nc.scalar.activation(root[:, pair], den[u][:], ACT.Abs_reciprocal_sqrt, bias=0.5)
+            squarer.tensor_tensor(recip[:, pair], root[:, pair], root[:, pair], ALU.mult)
 
-        a_ps = [ps.tile([P, 2 * S], F32, name="a_ps%d" % u) for u in range(2)]
-        for t in range(PACK):
-            product(a_ps[t // 2][:, S * (t % 2) : S * (t % 2 + 1)], cand_w, cand_s, t, z_w, z_s)
-        a_n3 = sb.tile([P, PACK * S], F32, name="a_n3")
-        diff = sb.tile([P, PACK * S], F32, name="diff")
-        res = sb.tile([P, PACK * S], F32, name="res")
-        half = sb.tile([P, PACK * S], F32, name="half")
-        out_rows = out_0.rearrange("(p t) j -> p t j", t=PACK)
-        for u in range(2):
-            nc.scalar.activation(a_all[:, 2 * S * u : 2 * S * (u + 1)], a_ps[u][:], ACT.Copy, scale=SIXTEENTH)
-        for t in range(PACK):
-            cols = slice(S * t, S * (t + 1))
-            nc.scalar.activation(a_n3[:, cols], a_all[:, S * t : S * t + WIN].indirect(n3_l[:]), ACT.Copy)
-            nc.vector.tensor_tensor(diff[:, cols], a_all[:, cols], a_n3[:, cols], ALU.subtract)
-            nc.vector.tensor_tensor(half[:, cols], diff[:, cols], root[:, cols], ALU.mult)
-            nc.vector.tensor_tensor(res[:, cols], half[:, cols], root[:, cols], ALU.mult)
-            nc.sync.dma_start(out_rows[:, t, :], res[:, cols])
+        a_n3 = [sb.tile([P, 2 * S], F32, name="a_n3_%d" % u, tag="den%d" % u) for u in range(2)]
+        diff = sb.tile([P, SLOTS * S], F32, name="diff")
+        res = sb.tile([P, SLOTS * S], F32, name="res")
+        out_rows = out_0.rearrange("(p t) j -> p t j", t=SLOTS)
+        for t in range(SLOTS):
+            nc.vector.tensor_scalar(a_val[:, slot(t)], a_ps[t][:], SIXTEENTH, None, ALU.mult)
+        for t in range(SLOTS):
+            other = a_n3[t // 2][:, slot(t % 2)]
+            nc.scalar.activation(other, a_val[:, slot(t, 2)].indirect(n3_l[:]), ACT.Copy)
+            nc.vector.scalar_tensor_tensor(diff[:, slot(t)], a_ps[t][:], SIXTEENTH, other, ALU.mult, ALU.subtract)
+            nc.vector.tensor_tensor(res[:, slot(t)], diff[:, slot(t)], recip[:, slot(t)], ALU.mult)
+            nc.sync.dma_start(out_rows[:, t, :], res[:, slot(t)])
 
-        res_woven = sb.tile([P, PACK * S], BF16, name="res_woven", align_bytes=64)
-        weave(res_woven, res)
+        res_woven = sb.tile([P, SLOTS * S], BF16, name="res_woven", align_bytes=64)
+        woven_groups = res_woven[:].rearrange("p (c i t) -> p c t i", t=SLOTS, i=LINE // 4)
+        res_groups = res[:].rearrange("p (t c i) -> p c t i", t=SLOTS, i=LINE // 4)
+        nc.vector.tensor_copy(woven_groups[:, :WEAVE_ON_VECTOR], res_groups[:, :WEAVE_ON_VECTOR])
+        nc.scalar.copy(woven_groups[:, WEAVE_ON_VECTOR:], res_groups[:, WEAVE_ON_VECTOR:])
         res_w = sb.tile([P, S], I32, name="res_w", align_bytes=64)
         res_s = sb.tile([P, S], U8, name="res_s", align_bytes=64)
         nc.vector.quantize_mx(out=res_w[:].bitcast(FP8X4), scales=res_s[:], in_=res_woven[:])
         nc.sync.dma_start(out_1[0].rearrange("p n t -> p (n t)").bitcast(I32), res_w[:])
         scale_rows = out_2[0].bitcast(I32)
-        for q in range(PACK):
+        for q in range(SLOTS):
             queue = nc.scalar if q % 2 == 0 else nc.sync
-            queue.dma_start(scale_rows[PACK * q : PACK * (q + 1), :], res_s[QUAD * q : QUAD * q + PACK, :].bitcast(I32))
+            queue.dma_start(scale_rows[SLOTS * q : SLOTS * (q + 1), :], res_s[QUAD * q : QUAD * q + SLOTS, :].bitcast(I32))

@@ -22,9 +22,11 @@ BLOCK_PARTS = 8
 SCALE_ROWS = K // 32
 WINDOW = 2 * S
 LINE = 16
+LIST_ROWS = 16
 SIXTEENTH = 0.0625
-N4_ON_SCALAR = 3
-WEAVE_ON_VECTOR = 42
+HALF = S // 2
+N4_ON_SCALAR = 2
+WEAVE_ON_VECTOR = 22
 
 
 def tile_picked_pqcjnormbhopg_none_po_kernel(
@@ -169,7 +171,7 @@ def tile_picked_pqcjnormbhopg_none_po_kernel(
         a_ps = [ps.tile([P, S], F32, name="a_ps%d" % t, tag="h_ps%d" % t) for t in range(SLOTS)]
         product(a_ps, cand_w, cand_s, z_w, z_s)
 
-        b_n4 = [sb.tile([P, S], F32, name="b_n4_%d" % t) for t in range(SLOTS)]
+        b_n4 = sb.tile([P, SLOTS * S], F32, name="b_n4")
         den = [sb.tile([P, 2 * S], F32, name="den%d" % u, tag="den%d" % u) for u in range(2)]
         root = sb.tile([P, SLOTS * S], F32, name="root")
         recip = sb.tile([P, SLOTS * S], F32, name="recip")
@@ -178,37 +180,60 @@ def tile_picked_pqcjnormbhopg_none_po_kernel(
         for t in range(SLOTS):
             looked_up = b_abs[:, slot(t, 2)].indirect(n4_l[:])
             if t < N4_ON_SCALAR:
-                nc.scalar.activation(b_n4[t][:], looked_up, ACT.Copy)
+                nc.scalar.activation(b_n4[:, slot(t)], looked_up, ACT.Copy)
             else:
-                nc.vector.tensor_copy(b_n4[t][:], looked_up)
-            nc.vector.tensor_tensor(den[t // 2][:, slot(t % 2)], b_abs[:, slot(t)], b_n4[t][:], ALU.add)
+                nc.vector.tensor_copy(b_n4[:, slot(t)], looked_up)
+            if t % 2 == 1:
+                adder = nc.gpsimd if t < N4_ON_SCALAR else nc.vector
+                adder.tensor_tensor(den[t // 2][:], b_abs[:, slot(t - 1, 2)], b_n4[:, slot(t - 1, 2)], ALU.add)
         for u, squarer in enumerate((nc.vector, nc.gpsimd)):
             pair = slot(2 * u, 2)
             nc.scalar.activation(root[:, pair], den[u][:], ACT.Abs_reciprocal_sqrt, bias=0.5)
             squarer.tensor_tensor(recip[:, pair], root[:, pair], root[:, pair], ALU.mult)
 
-        a_n3 = [sb.tile([P, 2 * S], F32, name="a_n3_%d" % u, tag="den%d" % u) for u in range(2)]
+        a_n3_first = sb.tile([P, S], F32, name="a_n3_first", tag="den0")
+        a_n3_rest = sb.tile([P, (SLOTS - 1) * S], F32, name="a_n3_rest", tag="den1")
+        a_n3 = [a_n3_first[:]] + [a_n3_rest[:, slot(t)] for t in range(SLOTS - 1)]
         diff = sb.tile([P, SLOTS * S], F32, name="diff")
         res = sb.tile([P, SLOTS * S], F32, name="res")
         out_rows = out_0.rearrange("(p t) j -> p t j", t=SLOTS)
         for t in range(SLOTS):
             nc.vector.tensor_scalar(a_val[:, slot(t)], a_ps[t][:], SIXTEENTH, None, ALU.mult)
-        for t in range(SLOTS):
-            other = a_n3[t // 2][:, slot(t % 2)]
-            nc.scalar.activation(other, a_val[:, slot(t, 2)].indirect(n3_l[:]), ACT.Copy)
-            nc.vector.scalar_tensor_tensor(diff[:, slot(t)], a_ps[t][:], SIXTEENTH, other, ALU.mult, ALU.subtract)
-            nc.vector.tensor_tensor(res[:, slot(t)], diff[:, slot(t)], recip[:, slot(t)], ALU.mult)
-            nc.sync.dma_start(out_rows[:, t, :], res[:, slot(t)])
+
+        def finish(t, first, last):
+            cols = slice(S * t + first, S * t + last)
+            other = a_n3[t][:, first:last]
+            entries = n3_l[:, first // LIST_ROWS : last // LIST_ROWS]
+            nc.scalar.activation(other, a_val[:, slot(t, 2)].indirect(entries), ACT.Copy)
+            nc.vector.scalar_tensor_tensor(diff[:, cols], a_ps[t][:, first:last], SIXTEENTH, other, ALU.mult, ALU.subtract)
+            nc.vector.tensor_tensor(res[:, cols], diff[:, cols], recip[:, cols], ALU.mult)
+            if last == S:
+                nc.sync.dma_start(out_rows[:, t, :], res[:, slot(t)])
+
+        for t in range(SLOTS - 1):
+            finish(t, 0, S)
 
         res_woven = sb.tile([P, SLOTS * S], BF16, name="res_woven", align_bytes=64)
         woven_groups = res_woven[:].rearrange("p (c i t) -> p c t i", t=SLOTS, i=LINE // 4)
         res_groups = res[:].rearrange("p (t c i) -> p c t i", t=SLOTS, i=LINE // 4)
-        nc.vector.tensor_copy(woven_groups[:, :WEAVE_ON_VECTOR], res_groups[:, :WEAVE_ON_VECTOR])
-        nc.scalar.copy(woven_groups[:, WEAVE_ON_VECTOR:], res_groups[:, WEAVE_ON_VECTOR:])
         res_w = sb.tile([P, S], I32, name="res_w", align_bytes=64)
         res_s = sb.tile([P, S], U8, name="res_s", align_bytes=64)
-        nc.vector.quantize_mx(out=res_w[:].bitcast(FP8X4), scales=res_s[:], in_=res_woven[:])
-        nc.sync.dma_start(out_1[0].rearrange("p n t -> p (n t)").bitcast(I32), res_w[:])
+        word_rows = out_1[0].rearrange("p n t -> p (n t)").bitcast(I32)
+        groups = HALF // (LINE // 4)
+        for half, on_vector in enumerate((groups, WEAVE_ON_VECTOR)):
+            first, last = HALF * half, HALF * (half + 1)
+            finish(SLOTS - 1, first, last)
+            by_vector = slice(groups * half, groups * half + on_vector)
+            nc.vector.tensor_copy(woven_groups[:, by_vector], res_groups[:, by_vector])
+            if on_vector < groups:
+                by_scalar = slice(groups * half + on_vector, groups * (half + 1))
+                nc.scalar.copy(woven_groups[:, by_scalar], res_groups[:, by_scalar])
+            nc.vector.quantize_mx(
+                out=res_w[:, first:last].bitcast(FP8X4),
+                scales=res_s[:, first:last],
+                in_=res_woven[:, SLOTS * first : SLOTS * last],
+            )
+            nc.sync.dma_start(word_rows[:, first:last], res_w[:, first:last])
         scale_rows = out_2[0].bitcast(I32)
         for q in range(SLOTS):
             queue = nc.scalar if q % 2 == 0 else nc.sync

from contextlib import ExitStack

import concourse.mybir as mybir

K, T, S, G, H, C = 512, 1024, 256, 2048, 512, 512
FLOPS = 3 * 2 * K * H * S

F32 = mybir.dt.float32
BF16 = mybir.dt.bfloat16
I32 = mybir.dt.int32
U32 = mybir.dt.uint32
U16 = mybir.dt.uint16
U8 = mybir.dt.uint8
FP8X4 = mybir.dt.float8_e4m3fn_x4
ACT = mybir.ActivationFunctionType
ALU = mybir.AluOpType

P = 128
SLOTS = 4
QUAD = 32
BLOCK_PARTS = 8
SCALE_ROWS = K // 32
WINDOW = 2 * S
LINE = 16
LIST_ROWS = 16
SIXTEENTH = 0.0625
HALF = S // 2
N4_ON_SCALAR = 2
WEAVE_ON_VECTOR = 22


def tile_picked_pqcjnormbhopg_none_po_kernel(
    tc, x_words, x_scales, d_words, d_scales, gs, offs, k1, n1, n2, cand, two, k2, n3, n4, out_0, out_1, out_2
):
    nc = tc.nc
    with ExitStack() as ctx:
        lists = ctx.enter_context(tc.tile_pool(name="lists", bufs=1))
        sb = ctx.enter_context(tc.tile_pool(name="sb", bufs=1))
        shared = ctx.enter_context(tc.tile_pool(name="shared", bufs=1))
        ps = ctx.enter_context(tc.psum_pool(name="ps", bufs=1))

        def slot(t, count=1):
            return slice(S * t, S * (t + count))

        def load_list(src, name):
            dst = lists.tile([P, src.shape[1]], U16, name=name)
            nc.sync.dma_start(dst[:], src)
            return dst

        d_w = sb.tile([P, G], I32, name="d_w", align_bytes=64)
        x_w = sb.tile([P, T], I32, name="x_w", align_bytes=64)
        d_s = sb.tile([P, G], U8, name="d_s", align_bytes=64)
        x_s = sb.tile([P, T], U8, name="x_s", align_bytes=64)

        k1_l = load_list(k1, "k1_l")
        d_rows = d_scales[0].bitcast(I32)
        nc.sync.dma_start(d_s[:].bitcast(I32), d_rows.unsqueeze(1).to_broadcast([SCALE_ROWS, BLOCK_PARTS, G // 4]))

        x_rows = x_scales[0].bitcast(I32)

        def load_x_scales(q, queue):
            rows = x_rows[SLOTS * q : SLOTS * (q + 1), :].unsqueeze(0).to_broadcast([QUAD // SLOTS, SLOTS, T // 4])
            queue.dma_start(x_s[QUAD * q : QUAD * (q + 1), :].bitcast(I32), rows)

        nc.scalar.dma_start(x_w[:], x_words[0].rearrange("p n t -> p (n t)").bitcast(I32))
        load_x_scales(0, nc.scalar)
        nc.scalar.dma_start(d_w[:], d_words[0].rearrange("p n t -> p (n t)").bitcast(I32))
        offs_l = load_list(offs, "offs_l")
        for q in range(1, SLOTS):
            load_x_scales(q, nc.sync)
        n1_l = load_list(n1, "n1_l")
        k2_l = load_list(k2, "k2_l")
        two_l = load_list(two, "two_l")
        n2_l = load_list(n2, "n2_l")
        cand_l = load_list(cand, "cand_l")
        n4_l = load_list(n4, "n4_l")
        n3_l = load_list(n3, "n3_l")

        gs_raw = sb.tile([P, SLOTS], F32, name="gs_raw")
        nc.gpsimd.dma_start(gs_raw[:], gs.rearrange("(p t) o -> p (t o)", t=SLOTS))
        gs_16th = sb.tile([P, SLOTS], F32, name="gs_16th")
        nc.gpsimd.tensor_scalar(gs_16th[:], gs_raw[:], SIXTEENTH, 0.0, ALU.mult, ALU.add)

        k1_s = sb.tile([P, H], U8, name="k1_s", align_bytes=64)
        k2_s = sb.tile([P, H], U8, name="k2_s", align_bytes=64)
        nc.vector.memset(k1_s[:].bitcast(I32), 0)
        nc.vector.memset(k2_s[:].bitcast(I32), 0)
        sig = [sb.tile([P, WINDOW], F32, name="sig%d" % t, tag="sig%d" % t, align_bytes=64) for t in range(SLOTS)]
        for t in range(SLOTS):
            nc.vector.memset(sig[t][:, S:], 0.0)
        b_abs = sb.tile([P, (SLOTS + 1) * S], F32, name="b_abs")
        a_val = sb.tile([P, (SLOTS + 1) * S], F32, name="a_val")
        nc.vector.memset(b_abs[:, slot(SLOTS)], 0.0)
        nc.vector.memset(a_val[:, slot(SLOTS)], 0.0)

        def gather_words(got, table, offsets):
            nc.vector.tensor_copy(got[:].bitcast(U32), table[:].bitcast(U32).indirect(offsets[:]))
            return got

        def gather_bytes(got, table, offsets):
            nc.vector.tensor_copy(got[:], table[:].indirect(offsets[:]))
            return got

        def deal(got, dtype, per_line, name):
            dealt = sb.tile([P, H], dtype, name=name, align_bytes=64)
            nc.vector.tensor_copy(
                dealt[:].rearrange("p (t c i) -> p c t i", t=SLOTS, i=per_line),
                got[:].rearrange("p (c i t) -> p c t i", t=SLOTS, i=per_line),
            )
            return dealt

        def place_scales(placed, dealt, queue):
            for i in range(SLOTS):
                queue.dma_start(placed[i:P:QUAD, :].bitcast(I32), dealt[BLOCK_PARTS * i : P : QUAD, :].bitcast(I32))

        def product(acc, w_words, w_scales, m_words, m_scales):
            for t in range(SLOTS):
                cols = slice(P * t, P * (t + 1))
                nc.tensor.matmul_mx(
                    out=acc[t][:],
                    lhsT=w_words[:, cols].bitcast(FP8X4),
                    lhsT_scale=w_scales[:, cols],
                    rhs=m_words[:].bitcast(FP8X4),
                    rhs_scale=m_scales[:],
                    start=True,
                    stop=True,
                )

        k1_s_got = gather_bytes(sb.tile([P, H], U8, name="k1_s_got", align_bytes=64), d_s, k1_l)
        place_scales(k1_s, deal(k1_s_got, U8, LINE, "k1_s_dealt"), nc.scalar)
        xq_w = gather_words(sb.tile([P, S], I32, name="xq_w", align_bytes=64), x_w, offs_l)
        k1_w_got = gather_words(shared.tile([P, H], I32, name="k1_w_got", align_bytes=64, offset=0), d_w, k1_l)
        k1_w = deal(k1_w_got, I32, LINE // 4, "k1_w")
        xq_s = gather_bytes(sb.tile([P, S], U8, name="xq_s", align_bytes=64), x_s, offs_l)
        h_ps = [ps.tile([P, S], F32, name="h_ps%d" % t, tag="h_ps%d" % t) for t in range(SLOTS)]
        product(h_ps, k1_w, k1_s, xq_w, xq_s)

        st = [sb.tile([P, WINDOW], F32, name="st%d" % t, tag="st%d" % t, align_bytes=64) for t in range(SLOTS)]
        nc.scalar.activation(sig[0][:, :S], h_ps[0][:], ACT.Sigmoid, scale=SIXTEENTH)
        for t in range(SLOTS):
            if t + 1 < SLOTS:
                nc.scalar.activation(sig[t + 1][:, :S], h_ps[t + 1][:], ACT.Sigmoid, scale=SIXTEENTH)
            nc.scalar.activation(st[t][:, S:], sig[t][:].indirect(n1_l[:]), ACT.Copy)
            nc.vector.scalar_tensor_tensor(st[t][:, :S], h_ps[t][:], gs_16th[:, t : t + 1], st[t][:, S:], ALU.mult, ALU.mult)

        k2_s_got = gather_bytes(shared.tile([P, H], U8, name="k2_s_got", align_bytes=64, offset=0), d_s, k2_l)
        place_scales(k2_s, deal(k2_s_got, U8, LINE, "k2_s_dealt"), nc.sync)
        x2_s = gather_bytes(shared.tile([P, S], U8, name="x2_s", align_bytes=64, offset=H), x_s, two_l)
        x2_w = gather_words(shared.tile([P, S], I32, name="x2_w", align_bytes=64, offset=2 * H), x_w, two_l)
        k2_w_got = gather_words(sb.tile([P, H], I32, name="k2_w_got", tag="sig0", align_bytes=64), d_w, k2_l)
        k2_w = deal(k2_w_got, I32, LINE // 4, "k2_w")
        b_ps = [ps.tile([P, S], F32, name="b_ps%d" % t) for t in range(SLOTS)]
        product(b_ps, k2_w, k2_s, x2_w, x2_s)

        st_n2 = sb.tile([P, SLOTS * S], F32, name="st_n2")
        z_woven = sb.tile([P, SLOTS * S], BF16, name="z_woven", align_bytes=64)
        z_slots = z_woven[:].rearrange("p (j t) -> p t j", t=SLOTS)
        for t in range(SLOTS):
            nc.scalar.activation(st_n2[:, slot(t)], st[t][:].indirect(n2_l[:]), ACT.Copy)
            nc.gpsimd.tensor_tensor(z_slots[:, t, :], st[t][:, :S], st_n2[:, slot(t)], ALU.subtract)

        cand_s_got = gather_bytes(sb.tile([P, C], U8, name="cand_s_got", tag="st1", align_bytes=64), x_s, cand_l)
        cand_s = deal(cand_s_got, U8, LINE, "cand_s")
        cand_w = sb.tile([P, C], I32, name="cand_w", tag="st0", align_bytes=64)
        nc.vector.tensor_copy(
            cand_w[:].bitcast(U32).rearrange("p (t m) -> p m t", t=SLOTS), x_w[:].bitcast(U32).indirect(cand_l[:])
        )
        z_w = sb.tile([P, S], I32, name="z_w", align_bytes=64)
        z_s = sb.tile([P, S], U8, name="z_s", align_bytes=64)
        nc.vector.quantize_mx(out=z_w[:].bitcast(FP8X4), scales=z_s[:], in_=z_woven[:])
        a_ps = [ps.tile([P, S], F32, name="a_ps%d" % t, tag="h_ps%d" % t) for t in range(SLOTS)]
        product(a_ps, cand_w, cand_s, z_w, z_s)

        b_n4 = sb.tile([P, SLOTS * S], F32, name="b_n4")
        den = [sb.tile([P, 2 * S], F32, name="den%d" % u, tag="den%d" % u) for u in range(2)]
        root = sb.tile([P, SLOTS * S], F32, name="root")
        recip = sb.tile([P, SLOTS * S], F32, name="recip")
        for t in range(SLOTS):
            nc.scalar.activation(b_abs[:, slot(t)], b_ps[t][:], ACT.Abs, scale=SIXTEENTH)
        for t in range(SLOTS):
            looked_up = b_abs[:, slot(t, 2)].indirect(n4_l[:])
            if t < N4_ON_SCALAR:
                nc.scalar.activation(b_n4[:, slot(t)], looked_up, ACT.Copy)
            else:
                nc.vector.tensor_copy(b_n4[:, slot(t)], looked_up)
            if t % 2 == 1:
                adder = nc.gpsimd if t < N4_ON_SCALAR else nc.vector
                adder.tensor_tensor(den[t // 2][:], b_abs[:, slot(t - 1, 2)], b_n4[:, slot(t - 1, 2)], ALU.add)
        for u, squarer in enumerate((nc.vector, nc.gpsimd)):
            pair = slot(2 * u, 2)
            nc.scalar.activation(root[:, pair], den[u][:], ACT.Abs_reciprocal_sqrt, bias=0.5)
            squarer.tensor_tensor(recip[:, pair], root[:, pair], root[:, pair], ALU.mult)

        a_n3_first = sb.tile([P, S], F32, name="a_n3_first", tag="den0")
        a_n3_rest = sb.tile([P, (SLOTS - 1) * S], F32, name="a_n3_rest", tag="den1")
        a_n3 = [a_n3_first[:]] + [a_n3_rest[:, slot(t)] for t in range(SLOTS - 1)]
        diff = sb.tile([P, SLOTS * S], F32, name="diff")
        res = sb.tile([P, SLOTS * S], F32, name="res")
        out_rows = out_0.rearrange("(p t) j -> p t j", t=SLOTS)
        for t in range(SLOTS):
            nc.vector.tensor_scalar(a_val[:, slot(t)], a_ps[t][:], SIXTEENTH, None, ALU.mult)

        def finish(t, first, last):
            cols = slice(S * t + first, S * t + last)
            other = a_n3[t][:, first:last]
            entries = n3_l[:, first // LIST_ROWS : last // LIST_ROWS]
            nc.scalar.activation(other, a_val[:, slot(t, 2)].indirect(entries), ACT.Copy)
            nc.vector.scalar_tensor_tensor(diff[:, cols], a_ps[t][:, first:last], SIXTEENTH, other, ALU.mult, ALU.subtract)
            nc.vector.tensor_tensor(res[:, cols], diff[:, cols], recip[:, cols], ALU.mult)
            if last == S:
                nc.sync.dma_start(out_rows[:, t, :], res[:, slot(t)])

        for t in range(SLOTS - 1):
            finish(t, 0, S)

        res_woven = sb.tile([P, SLOTS * S], BF16, name="res_woven", align_bytes=64)
        woven_groups = res_woven[:].rearrange("p (c i t) -> p c t i", t=SLOTS, i=LINE // 4)
        res_groups = res[:].rearrange("p (t c i) -> p c t i", t=SLOTS, i=LINE // 4)
        res_w = sb.tile([P, S], I32, name="res_w", align_bytes=64)
        res_s = sb.tile([P, S], U8, name="res_s", align_bytes=64)
        word_rows = out_1[0].rearrange("p n t -> p (n t)").bitcast(I32)
        groups = HALF // (LINE // 4)
        for half, on_vector in enumerate((groups, WEAVE_ON_VECTOR)):
            first, last = HALF * half, HALF * (half + 1)
            finish(SLOTS - 1, first, last)
            by_vector = slice(groups * half, groups * half + on_vector)
            nc.vector.tensor_copy(woven_groups[:, by_vector], res_groups[:, by_vector])
            if on_vector < groups:
                by_scalar = slice(groups * half + on_vector, groups * (half + 1))
                nc.scalar.copy(woven_groups[:, by_scalar], res_groups[:, by_scalar])
            nc.vector.quantize_mx(
                out=res_w[:, first:last].bitcast(FP8X4),
                scales=res_s[:, first:last],
                in_=res_woven[:, SLOTS * first : SLOTS * last],
            )
            nc.sync.dma_start(word_rows[:, first:last], res_w[:, first:last])
        scale_rows = out_2[0].bitcast(I32)
        for q in range(SLOTS):
            queue = nc.scalar if q % 2 == 0 else nc.sync
            queue.dma_start(scale_rows[SLOTS * q : SLOTS * (q + 1), :], res_s[QUAD * q : QUAD * q + SLOTS, :].bitcast(I32))
